import numpy as np, ml_dtypes
CORES = [3,7,11,15,131,135,139,143]
N = 8
import mx_ref
BF = ml_dtypes.bfloat16
def entries(a):
    return np.ascontiguousarray(a.T).reshape(-1)
def table(e):
    return np.ascontiguousarray(np.reshape(e, (-1, 16)).T).astype(np.int32)
def cut(t, i, w=512):
    return t[:, w * i:w * i + w]
def f(rng, *shape):
    return mx_ref.flush((rng.standard_normal(shape, dtype=np.float32) * np.exp2(rng.integers(-2, 3, shape[:-1] + (1,)))).astype(BF))
def wide(rng, *shape, cols=0):
    v = rng.standard_normal(shape, dtype=np.float32) * np.exp2(rng.integers(-12, 13, shape)).astype(np.float32)
    if cols: v *= np.repeat(np.exp2(rng.integers(-cols, cols + 1, shape[:-2] + (1, shape[-1] // 4))) * (rng.random(shape[:-2] + (1, shape[-1] // 4)) > 0.0625), 4, axis=-1).astype(np.float32)
    return mx_ref.flush(v.astype(BF))
PG, NW, SP, CW, CP, O = 16, 64, 16, 16, 4, 2
def counts(rng, total, cap, least):
    n = np.array(least)
    while n.sum() < total: n[rng.choice(np.flatnonzero(n < cap))] += 1
    return n
def lists(rng, full=False, own=False, shared=False, rewritten=False):
    h = int(rng.integers(0, N)); hot = rng.permutation(PG)[:CP if shared else 2]
    fr, pg = np.zeros((N, SP), int), np.zeros((N, SP), int)
    rd, wr, wp = np.full((N, N * CP), -1), np.full((N, N * CW), -1), np.full((N, N * CW), -1)
    for s in range(N):
        lw, lp = np.zeros(N, int), np.zeros(N, int)
        if full:
            a = np.append(h, rng.permutation(np.delete(np.arange(N), h)))
            lw[a[:NW // CW]] = CW; lp[a[:SP // CP]] = CP
        if own: lw[s] = CW; lp[s] = CP
        if shared: lw[h] = CW; lp[h] = CP
        if rewritten: lw[h] = CW; lp[h] = 1
        n, fresh, at = counts(rng, NW, CW, lw), rng.permutation(NW), 0
        for q in range(N):
            c = rng.permutation(CW)[:n[q]]
            wr[s, q * CW + c] = fresh[at:at + n[q]]; wp[q, s * CW + c] = 0; at += n[q]
        n, slots, frames = counts(rng, SP, CP, lp), [], []
        for q in range(N):
            must = np.zeros(0, int)
            if q == h and shared: must = hot
            if q == h and rewritten: must = hot[s % 2:s % 2 + 1]
            g = np.concatenate([must, rng.permutation(np.setdiff1d(np.arange(PG), must))])[:n[q]]
            c = rng.permutation(CP)[:n[q]]
            rd[q, s * CP + c] = g; slots.append(q * CP + c); frames.append(q * PG + g)
        o = rng.permutation(SP)
        pg[s] = np.concatenate(slots)[o]; fr[s] = np.concatenate(frames)[o]
    for q in range(N):
        k = np.flatnonzero(wp[q] >= 0); must = np.zeros(0, int)
        if q == h and shared: must = 16 * hot + rng.integers(0, 16, hot.size)
        if q == h and rewritten: must = (16 * hot[:, None] + np.arange(16)).reshape(-1)
        p = np.concatenate([must, rng.permutation(np.setdiff1d(np.arange(16 * PG), must))])[:k.size]
        wp[q, k] = rng.permutation(p)
    return {n: np.stack([table(v) for v in a]) for n, a in (("fr", fr), ("wr", wr), ("wp", wp), ("rd", rd), ("pg", pg))}
def setup_inputs(rng):
    return {"pl": f(rng, N, 128, 64 * PG), "nw": f(rng, N, 128, 4 * NW), "qw": f(rng, N, 128, 512 * O), **lists(rng)}
def setup_inputs_full(rng):
    return {**setup_inputs(rng), **lists(rng, full=True)}
def setup_inputs_own(rng):
    return {**setup_inputs(rng), **lists(rng, own=True)}
def setup_inputs_rewritten(rng):
    return {**setup_inputs(rng), **lists(rng, rewritten=True)}
def setup_inputs_shared(rng):
    return {**setup_inputs(rng), **lists(rng, shared=True)}
def setup_inputs_spread(rng):
    d = setup_inputs(rng); d["pl"] = wide(rng, N, 128, 64 * PG, cols=8); d["nw"] = wide(rng, N, 128, 4 * NW, cols=8); return d
def check_inputs(d):
    b = []
    for r in range(N):
        t, a, p, k, g = [entries(d[n][r]) for n in ("fr", "wr", "wp", "rd", "pg")]
        if t.min() < 0 or t.max() >= N * PG or len(set(t.tolist())) != SP: b.append("fr")
        if a.min() < -1 or a.max() >= NW or sorted(a[a >= 0].tolist()) != list(range(NW)): b.append("wr")
        sent = np.concatenate([entries(d["wr"][s])[r * CW:r * CW + CW] for s in range(N)]); v = p[p >= 0]
        if p.min() < -1 or p.max() >= 16 * PG or len(set(v.tolist())) != v.size or ((p >= 0) != (sent >= 0)).any(): b.append("wp")
        if k.min() < -1 or k.max() >= PG: b.append("rd")
        got = np.concatenate([entries(d["rd"][q])[r * CP:r * CP + CP] for q in range(N)])
        if g.min() < 0 or g.max() >= N * CP or len(set(g.tolist())) != SP or (got >= 0).sum() != SP: b.append("pg")
        elif (got[g] < 0).any() or (g // CP * PG + got[g] != t).any(): b.append("pg")
    return b
def reference(pl, nw, qw, fr, wr, wp, rd, pg):
    pools = []
    for q in range(N):
        v = pl[q].reshape(128, 16 * PG, 4).copy()
        for s in range(N):
            c, p = entries(wr[s])[q * CW:q * CW + CW], entries(wp[q])[s * CW:s * CW + CW]
            k = p >= 0
            v[:, p[k]] = nw[s].reshape(128, NW, 4)[:, c[k]]
        pools.append(v)
    pools = np.concatenate(pools, axis=1)
    y = np.zeros((N, 128, O * SP * 16), np.float32)
    for r in range(N):
        e = (16 * entries(fr[r])[:, None] + np.arange(16)).reshape(-1)
        pages = mx_ref.quantize(np.ascontiguousarray(pools[:, e]).reshape(128, -1))
        for o in range(O):
            y[r][:, SP * 16 * o:SP * 16 * o + SP * 16] = mx_ref.matmul(mx_ref.quantize(np.ascontiguousarray(cut(qw[r], o))), pages)
    return {"y": y}

@@ -1,0 +1,220 @@
+from concourse.bass import DstId, RemoteDMATransfer
+from concourse.mybir import dt, AluOpType, ActivationFunctionType
+
+N, PG, NW, SP, CW, CP, O = 8, 16, 64, 16, 16, 4, 2
+POOL = 16 * PG
+PAGE = 16 * CP
+F8 = "float8_e4m3fn_x4"
+
+SCRATCH = {
+    "nwt": ("sbuf", [128, 512], "bfloat16"),
+    "plt": ("sbuf", [128, 4 * POOL], "bfloat16"),
+    "qwt": ("sbuf", [128, 512 * O], "bfloat16"),
+    "nwq": ("sbuf", [128, 128], F8), "nws": ("sbuf", [128, 128], "uint8"),
+    "qwq": ("sbuf", [128, 128 * O], F8), "qws": ("sbuf", [128, 128 * O], "uint8"),
+    "slot1": ("sbuf", [128, N * CW], F8), "slot1s": ("sbuf", [128, N * CW], "uint8"),
+    "win": ("sbuf", [128, POOL + N * CW], F8), "wins": ("sbuf", [128, POOL + N * CW], "uint8"),
+    "slot2": ("sbuf", [128, N * PAGE], F8), "slot2s": ("sbuf", [128, N * PAGE], "uint8"),
+    "land2": ("sbuf", [128, N * PAGE], F8), "land2s": ("sbuf", [128, N * PAGE], "uint8"),
+    "fin": ("sbuf", [128, POOL], F8), "fins": ("sbuf", [128, POOL], "uint8"),
+    "wrt": ("sbuf", [128, N * CW // 16], "int32"),
+    "wpt": ("sbuf", [128, N * CW // 16], "int32"),
+    "rdt": ("sbuf", [128, N * CP // 16], "int32"),
+    "pgrow": ("sbuf", [1, SP], "int32"), "pgb": ("sbuf", [128, SP], "int32"),
+    "cval": ("sbuf", [128, N * CW], "float32"),
+    "cdmp": ("sbuf", [128, N * CW // 16], "int32"),
+    "cdif": ("sbuf", [128, POOL], "int32"), "cmod": ("sbuf", [128, POOL], "int32"), "cmask": ("sbuf", [128, POOL], "float32"),
+    "crow": ("sbuf", [128, 1], "int32"), "crow16": ("sbuf", [128, 1], "int32"), "crowf": ("sbuf", [128, 1], "float32"),
+    "wpa": ("sbuf", [128, N * CW // 16], "int32"), "wpb": ("sbuf", [128, N * CW // 16], "int32"),
+    "comp": ("sbuf", [128, 512], "float32"),
+    "fold0": ("sbuf", [128, 256], "float32"), "fold1": ("sbuf", [128, 128], "float32"), "fold2": ("sbuf", [128, 64], "float32"),
+    "fold3": ("sbuf", [128, 32], "float32"), "comp2": ("sbuf", [128, 16], "float32"),
+    "offw": ("sbuf", [128, N * CW // 16], "uint16"), "offo": ("sbuf", [128, 2], "uint16"),
+    "offp": ("sbuf", [128, N * CW // 16], "uint16"), "offr": ("sbuf", [128, N * CP // 16], "uint16"),
+    "list2": ("sbuf", [128, N * CP], "uint16"), "off3": ("sbuf", [128, SP], "uint16"),
+    "acc": ("psum", [128, 512 * 4], "float32"),
+    "yt": ("sbuf", [128, 256 * O], "float32"),
+}
+DMA_SEMS = ["d_nw", "d_wr", "d_pl", "d_wp", "d_rd", "d_pg", "d_qw", "d_y"]
+EVENTS = ["zero", "offw", "q_nw", "c1", "s1", "offo", "own_c", "own_s", "q_pl", "q_qw",
+          "i_comp", "i_val", "i_dmp", "i_dif", "i_row", "k_mod", "k_mask", "k_row", "k_rowf",
+          "k_wpa", "k_wpb", "k_offp", "k_comp", "k_f0", "k_f1", "k_f2", "k_f3", "k_f4", "k_offr", "k_list2", "pgb", "k_off3",
+          "c2", "s2", "own2_c", "own2_s", "fc0", "fc1", "fs0", "fs1",
+          "m00", "m01", "m10", "m11", "y0", "y1"]
+SEMAPHORES = DMA_SEMS + EVENTS + ["in_c1", "in_s1", "in_c2", "in_s2", "sent"]
+
+
+def plan(src, cores, topo):
+    peer = [d for d in cores if d != src and d in topo.cores_of(src)]
+    off = [d for d in cores if d not in topo.cores_of(src)]
+    near = [d for d in off if topo.mates(src, d)] + [d for d in off if topo.same_plane(src, d)]
+    far = [d for d in off if d not in near]
+    e = topo.engines(src, off[0])
+    a, b = e[0::2], e[1::2]
+    out = {}
+    for i, d in enumerate(near):
+        out[d] = ([a[i]], [b[i]])
+    for i, d in enumerate(far):
+        out[d] = (b[2 * i:2 * i + 2], a[2 * i:2 * i + 2])
+    for d in peer:
+        rest = [x for x in topo.engines(src, d) if x not in e]
+        out[d] = ([rest[0]], [rest[2]])
+    return out
+
+
+def rank_program(g, core, T, topo):
+    rank = T.rank_of(core)
+    if rank is None:
+        return
+    sem = T.sem
+    v, s, y, t = g.vector, g.scalar, g.sync, g.tensor
+    copy = ActivationFunctionType.Copy
+    cores = list(T.cores)
+    ways = plan(core, cores, topo)
+    came = [plan(d, cores, topo)[core] for d in cores if d != core]
+    n_codes, n_scales = sum(len(w[0]) for w in came), sum(len(w[1]) for w in came)
+
+    def wait(q, *names):
+        for n in names:
+            q.wait_ge(sem[n], 1)
+
+    y.dma_start(T.nwt[:, 0:4 * NW], T.nw[:]).then_inc(sem.d_nw, 16)
+    for k in range(8):
+        (y if k < 3 else s).dma_start(T.wrt[16 * k:16 * k + 16, :], T.wr[:]).then_inc(sem.d_wr, 16)
+    s.dma_start(T.plt[:], T.pl[:]).then_inc(sem.d_pl, 16)
+    for k in range(8):
+        y.dma_start(T.wpt[16 * k:16 * k + 16, :], T.wp[:]).then_inc(sem.d_wp, 16)
+    for k in range(8):
+        y.dma_start(T.rdt[16 * k:16 * k + 16, :], T.rd[:]).then_inc(sem.d_rd, 16)
+    y.dma_start(T.pgrow[0:1, :], T.pg[:]).then_inc(sem.d_pg, 16)
+    y.dma_start(T.qwt[:], T.qw[:]).then_inc(sem.d_qw, 16)
+
+    fl = dict(allow_small_or_imprecise_dtypes=True)
+    g.iota(T.comp[:, 0:POOL], [[1, POOL]], 0, 0, **fl).then_inc(sem.i_comp, 1)
+    g.iota(T.cval[:], [[1, N * CW]], POOL, 0, **fl).then_inc(sem.i_val, 1)
+    g.iota(T.cdmp[:], [[16, N * CW // 16]], POOL, 1).then_inc(sem.i_dmp, 1)
+    g.iota(T.cdif[:], [[0, 16], [1, 16]], 128, -1).then_inc(sem.i_dif, 1)
+    g.iota(T.crow[:], [[0, 1]], 0, 1).then_inc(sem.i_row, 1)
+
+    v.memset(T.nwt[:, 4 * NW:512], 0.0).then_inc(sem.zero, 1)
+    v.wait_ge(sem.d_wr, 128)
+    v.tensor_copy(T.offw[:], T.wrt[:]).then_inc(sem.offw, 1)
+    v.wait_ge(sem.d_nw, 16)
+    wait(v, "zero")
+    v.quantize_mx(T.nwq[:], T.nws[:], T.nwt[:]).then_inc(sem.q_nw, 1)
+    wait(v, "offw", "q_nw")
+    v.tensor_copy(T.slot1[:, 0:N * CW].bitcast(dt.uint32), T.nwq[:, 0:NW].bitcast(dt.uint32).indirect(T.offw[:, 0:8])).then_inc(sem.c1, 1)
+    wait(s, "offw", "q_nw")
+    s.activation(T.slot1s[:, 0:N * CW], T.nws[:, 0:NW].indirect(T.offw[:, 0:8]), copy).then_inc(sem.s1, 1)
+
+    def send(src, dst, width, base, part, arrive):
+        tr = []
+        for d in sorted(ways, key=lambda c: (len(ways[c][0]) == 1, c)):
+            q = T.rank_of(d)
+            rid, pid = topo.addr(d, core)
+            a, b = src[:, width * q:width * q + width], dst[:, base + width * rank:base + width * rank + width]
+            if part == 0:
+                a, b = a.bitcast(dt.uint8), b.bitcast(dt.uint8)
+            tr.append(RemoteDMATransfer(dst_ids=[DstId(rid=rid, pnc=pid)], dma_engine_mask=sum(1 << e for e in ways[d][part]),
+                                        remote_sem=sem[arrive], src=a, dst=b))
+        g.remote_dma_fused(tr, local_sem=sem.sent)
+        return sum(len(ways[d][part]) for d in ways)
+
+    sent = 0
+    wait(g, "c1")
+    sent += send(T.slot1, T.win, CW, POOL, 0, "in_c1")
+    wait(g, "s1")
+    sent += send(T.slot1s, T.wins, CW, POOL, 1, "in_s1")
+
+    lo = POOL + CW * rank
+    v.tensor_copy(T.offo[:, 0:1], T.wrt[:, rank:rank + 1]).then_inc(sem.offo, 1)
+    wait(v, "offo")
+    v.tensor_copy(T.win[:, lo:lo + CW].bitcast(dt.uint32), T.nwq[:, 0:NW].bitcast(dt.uint32).indirect(T.offo[:, 0:1])).then_inc(sem.own_c, 1)
+    wait(s, "offo")
+    s.activation(T.wins[:, lo:lo + CW], T.nws[:, 0:NW].indirect(T.offo[:, 0:1]), copy).then_inc(sem.own_s, 1)
+
+    v.wait_ge(sem.d_pl, 16)
+    v.quantize_mx(T.win[:, 0:POOL], T.wins[:, 0:POOL], T.plt[:]).then_inc(sem.q_pl, 1)
+
+    wait(v, "i_dmp")
+    v.wait_ge(sem.d_wp, 128)
+    v.tensor_scalar(T.wpa[:], T.wpt[:], 4095, None, AluOpType.bitwise_and).then_inc(sem.k_wpa, 1)
+    wait(v, "i_dif")
+    v.tensor_scalar(T.cmod[:], T.cdif[:], 15, None, AluOpType.bitwise_and).then_inc(sem.k_mod, 1)
+    wait(v, "k_wpa")
+    v.tensor_tensor(T.wpb[:], T.wpa[:], T.cdmp[:], AluOpType.min).then_inc(sem.k_wpb, 1)
+    wait(v, "k_mod")
+    v.tensor_scalar(T.cmask[:], T.cmod[:], 0, None, AluOpType.is_equal).then_inc(sem.k_mask, 1)
+    wait(v, "k_wpb")
+    v.tensor_copy(T.offp[:], T.wpb[:]).then_inc(sem.k_offp, 1)
+    wait(v, "i_comp", "i_val", "k_offp")
+    v.tensor_copy(T.comp[:, 0:512].indirect(T.offp[:, 0:8]), T.cval[:]).then_inc(sem.k_comp, 1)
+    wait(v, "k_mask", "k_comp")
+    v.tensor_tensor(T.fold0[:], T.comp[:, 0:POOL], T.cmask[:], AluOpType.mult).then_inc(sem.k_f0, 1)
+    wait(v, "k_f0")
+    v.tensor_tensor(T.fold1[:], T.fold0[:, 0:256:2], T.fold0[:, 1:256:2], AluOpType.add).then_inc(sem.k_f1, 1)
+    wait(v, "k_f1")
+    v.tensor_tensor(T.fold2[:], T.fold1[:, 0:128:2], T.fold1[:, 1:128:2], AluOpType.add).then_inc(sem.k_f2, 1)
+    wait(v, "k_f2")
+    v.tensor_tensor(T.fold3[:], T.fold2[:, 0:64:2], T.fold2[:, 1:64:2], AluOpType.add).then_inc(sem.k_f3, 1)
+    v.wait_ge(sem.d_rd, 128)
+    v.tensor_copy(T.offr[:], T.rdt[:]).then_inc(sem.k_offr, 1)
+    wait(v, "k_f3")
+    v.tensor_tensor(T.comp2[:], T.fold3[:, 0:32:2], T.fold3[:, 1:32:2], AluOpType.add).then_inc(sem.k_f4, 1)
+    wait(v, "k_f4", "k_offr")
+    v.tensor_copy(T.list2[:], T.comp2[:, 0:16].indirect(T.offr[:, 0:2])).then_inc(sem.k_list2, 1)
+    wait(v, "i_row")
+    v.tensor_scalar(T.crow16[:], T.crow[:], 15, None, AluOpType.bitwise_and).then_inc(sem.k_row, 1)
+    v.wait_ge(sem.d_qw, 16)
+    v.quantize_mx(T.qwq[:], T.qws[:], T.qwt[:]).then_inc(sem.q_qw, 1)
+    wait(v, "k_row")
+    v.tensor_copy(T.crowf[:], T.crow16[:]).then_inc(sem.k_rowf, 1)
+    g.wait_ge(sem.d_pg, 16)
+    g.partition_broadcast(T.pgb[:], T.pgrow[0:1, :], 128).then_inc(sem.pgb, 1)
+    wait(v, "pgb", "k_rowf")
+    v.tensor_scalar(T.off3[:], T.pgb[:], 16.0, T.crowf[:, 0:1], AluOpType.mult, AluOpType.add).then_inc(sem.k_off3, 1)
+
+    wide = POOL + N * CW
+    parts = [(a, b) for a, b in ((0, rank), (rank + 1, N)) if a < b]
+    wait(v, "k_list2", "q_pl", "own_c")
+    v.wait_ge(sem.in_c1, n_codes)
+    for a, b in parts:
+        v.tensor_copy(T.slot2[:, PAGE * a:PAGE * b].bitcast(dt.uint32),
+                      T.win[:, 0:wide].bitcast(dt.uint32).indirect(T.list2[:, CP * a:CP * b])).then_inc(sem.c2, 1)
+    wait(s, "k_list2", "q_pl", "own_s")
+    s.wait_ge(sem.in_s1, n_scales)
+    for a, b in parts:
+        s.activation(T.slot2s[:, PAGE * a:PAGE * b], T.wins[:, 0:wide].indirect(T.list2[:, CP * a:CP * b]), copy).then_inc(sem.s2, 1)
+    g.wait_ge(sem.c2, len(parts))
+    sent += send(T.slot2, T.land2, PAGE, 0, 0, "in_c2")
+    g.wait_ge(sem.s2, len(parts))
+    sent += send(T.slot2s, T.land2s, PAGE, 0, 1, "in_s2")
+    own = (PAGE * rank, PAGE * rank + PAGE)
+    lst = T.list2[:, CP * rank:CP * rank + CP]
+    v.tensor_copy(T.land2[:, own[0]:own[1]].bitcast(dt.uint32), T.win[:, 0:wide].bitcast(dt.uint32).indirect(lst)).then_inc(sem.own2_c, 1)
+    s.activation(T.land2s[:, own[0]:own[1]], T.wins[:, 0:wide].indirect(lst), copy).then_inc(sem.own2_s, 1)
+
+    wait(v, "own2_c", "k_off3")
+    v.wait_ge(sem.in_c2, n_codes)
+    wait(s, "own2_s", "k_off3")
+    s.wait_ge(sem.in_s2, n_scales)
+    wait(t, "q_qw")
+    for h in range(2):
+        a, b, lst = 128 * h, 128 * h + 128, T.off3[:, 8 * h:8 * h + 8]
+        v.tensor_copy(T.fin[:, a:b].bitcast(dt.uint32), T.land2[:, 0:N * PAGE].bitcast(dt.uint32).indirect(lst)).then_inc(sem["fc%d" % h], 1)
+        s.activation(T.fins[:, a:b], T.land2s[:, 0:N * PAGE].indirect(lst), copy).then_inc(sem["fs%d" % h], 1)
+        wait(t, "fc%d" % h, "fs%d" % h)
+        for o in range(O):
+            t.matmul_mx(T.acc[:, 512 * (2 * o + h):512 * (2 * o + h) + 128], T.qwq[:, 128 * o:128 * o + 128], T.qws[:, 128 * o:128 * o + 128],
+                        T.fin[:, a:b], T.fins[:, a:b], True, True).then_inc(sem["m%d%d" % (o, h)], 1)
+    for h in range(2):
+        wait(v, "m0%d" % h)
+        v.tensor_copy(T.yt[:, 128 * h:128 * h + 128], T.acc[:, 512 * h:512 * h + 128]).then_inc(sem.y0, 1)
+        wait(s, "m1%d" % h)
+        s.activation(T.yt[:, 256 + 128 * h:256 + 128 * h + 128], T.acc[:, 1024 + 512 * h:1024 + 512 * h + 128], copy).then_inc(sem.y1, 1)
+    y.wait_ge(sem.y0, 2)
+    y.dma_start(T.y[:, 0:256], T.yt[:, 0:256]).then_inc(sem.d_y, 16)
+    s.wait_ge(sem.y1, 2)
+    s.dma_start(T.y[:, 256:512], T.yt[:, 256:512]).then_inc(sem.d_y, 16)
+    y.wait_ge(sem.d_y, 32)
+    g.wait_ge(sem.sent, sent)

@@ -4,6 +4,8 @@ from concourse.mybir import dt, AluOpType, ActivationFunctionType
 N, PG, NW, SP, CW, CP, O = 8, 16, 64, 16, 16, 4, 2
 POOL = 16 * PG
 PAGE = 16 * CP
+OWN = POOL + N * CW
+WIDE = OWN + 2 * CW
 F8 = "float8_e4m3fn_x4"
 
 SCRATCH = {
@@ -13,52 +15,67 @@ SCRATCH = {
     "nwq": ("sbuf", [128, 128], F8), "nws": ("sbuf", [128, 128], "uint8"),
     "qwq": ("sbuf", [128, 128 * O], F8), "qws": ("sbuf", [128, 128 * O], "uint8"),
     "slot1": ("sbuf", [128, N * CW], F8), "slot1s": ("sbuf", [128, N * CW], "uint8"),
-    "win": ("sbuf", [128, POOL + N * CW], F8), "wins": ("sbuf", [128, POOL + N * CW], "uint8"),
+    "win": ("sbuf", [128, WIDE], F8), "wins": ("sbuf", [128, WIDE], "uint8"),
     "slot2": ("sbuf", [128, N * PAGE], F8), "slot2s": ("sbuf", [128, N * PAGE], "uint8"),
     "land2": ("sbuf", [128, N * PAGE], F8), "land2s": ("sbuf", [128, N * PAGE], "uint8"),
     "fin": ("sbuf", [128, POOL], F8), "fins": ("sbuf", [128, POOL], "uint8"),
-    "wrt": ("sbuf", [128, N * CW // 16], "int32"),
-    "wpt": ("sbuf", [128, N * CW // 16], "int32"),
-    "rdt": ("sbuf", [128, N * CP // 16], "int32"),
+    "wrt": ("sbuf", [32, N * CW // 16], "int32"),
+    "wpt": ("sbuf", [32, N * CW // 16], "int32"),
+    "rdt": ("sbuf", [32, N * CP // 16], "int32"),
     "pgrow": ("sbuf", [1, SP], "int32"), "pgb": ("sbuf", [128, SP], "int32"),
     "cval": ("sbuf", [128, N * CW], "float32"),
     "cdmp": ("sbuf", [128, N * CW // 16], "int32"),
-    "cdif": ("sbuf", [128, POOL], "int32"), "cmod": ("sbuf", [128, POOL], "int32"), "cmask": ("sbuf", [128, POOL], "float32"),
-    "crow": ("sbuf", [128, 1], "int32"), "crow16": ("sbuf", [128, 1], "int32"), "crowf": ("sbuf", [128, 1], "float32"),
-    "wpa": ("sbuf", [128, N * CW // 16], "int32"), "wpb": ("sbuf", [128, N * CW // 16], "int32"),
+    "ccol": ("sbuf", [128, POOL], "float32"), "coff": ("sbuf", [128, POOL], "float32"),
+    "cmask": ("sbuf", [128, POOL], "float32"), "cnot": ("sbuf", [128, POOL], "float32"),
+    "crow": ("sbuf", [128, 1], "int32"), "crow16": ("sbuf", [128, 1], "int32"),
+    "crowp": ("sbuf", [128, 1], "float32"), "crowf": ("sbuf", [128, 1], "float32"), "crown": ("sbuf", [128, 1], "float32"),
+    "wpa": ("sbuf", [32, N * CW // 16], "int32"), "wpb": ("sbuf", [32, N * CW // 16], "int32"),
     "comp": ("sbuf", [128, 512], "float32"),
-    "fold0": ("sbuf", [128, 256], "float32"), "fold1": ("sbuf", [128, 128], "float32"), "fold2": ("sbuf", [128, 64], "float32"),
-    "fold3": ("sbuf", [128, 32], "float32"), "comp2": ("sbuf", [128, 16], "float32"),
-    "offw": ("sbuf", [128, N * CW // 16], "uint16"), "offo": ("sbuf", [128, 2], "uint16"),
+    "mine": ("sbuf", [128, POOL], "float32"), "last": ("sbuf", [128, POOL], "float32"),
+    "offw": ("sbuf", [128, N * CW // 16], "uint16"),
     "offp": ("sbuf", [128, N * CW // 16], "uint16"), "offr": ("sbuf", [128, N * CP // 16], "uint16"),
     "list2": ("sbuf", [128, N * CP], "uint16"), "off3": ("sbuf", [128, SP], "uint16"),
     "acc": ("psum", [128, 512 * 4], "float32"),
     "yt": ("sbuf", [128, 256 * O], "float32"),
 }
 DMA_SEMS = ["d_nw", "d_wr", "d_pl", "d_wp", "d_rd", "d_pg", "d_qw", "d_y"]
-EVENTS = ["zero", "offw", "q_nw", "c1", "s1", "offo", "own_c", "own_s", "q_pl", "q_qw",
-          "i_comp", "i_val", "i_dmp", "i_dif", "i_row", "k_mod", "k_mask", "k_row", "k_rowf",
-          "k_wpa", "k_wpb", "k_offp", "k_comp", "k_f0", "k_f1", "k_f2", "k_f3", "k_f4", "k_offr", "k_list2", "pgb", "k_off3",
-          "c2", "s2", "own2_c", "own2_s", "fc0", "fc1", "fs0", "fs1",
+EVENTS = ["zero", "offw", "q_nw", "c1", "s1", "own_c", "own_s", "q_pl", "q_qw",
+          "i_comp", "i_col", "i_row", "k_val", "k_dmp", "k_coff", "k_mask", "k_not", "k_row", "k_rowp", "k_rowf", "k_rown",
+          "k_wpa", "k_wpb", "k_offp", "k_comp", "k_mine", "k_last", "k_offr", "k_list2", "pgb", "k_off3",
+          "c2_0", "c2_1", "s2_0", "s2_1", "own2_c", "own2_s", "fc0", "fc1", "fs0", "fs1",
           "m00", "m01", "m10", "m11", "y0", "y1"]
 SEMAPHORES = DMA_SEMS + EVENTS + ["in_c1", "in_s1", "in_c2", "in_s2", "sent"]
 
 
-def plan(src, cores, topo):
+def kinds(src, cores, topo):
     peer = [d for d in cores if d != src and d in topo.cores_of(src)]
     off = [d for d in cores if d not in topo.cores_of(src)]
     near = [d for d in off if topo.mates(src, d)] + [d for d in off if topo.same_plane(src, d)]
-    far = [d for d in off if d not in near]
-    e = topo.engines(src, off[0])
+    return near, [d for d in off if d not in near], peer
+
+
+def plan(src, cores, topo):
+    near, far, peer = kinds(src, cores, topo)
+    e = topo.engines(src, near[0])
     a, b = e[0::2], e[1::2]
     out = {}
     for i, d in enumerate(near):
-        out[d] = ([a[i]], [b[i]])
+        out[d] = ([a[i]], [b[i]], e[2 * i:2 * i + 2])
     for i, d in enumerate(far):
-        out[d] = (b[2 * i:2 * i + 2], a[2 * i:2 * i + 2])
+        out[d] = (b[2 * i:2 * i + 2], a[2 * i:2 * i + 2], e[4 * i:4 * i + 4])
     for d in peer:
         rest = [x for x in topo.engines(src, d) if x not in e]
-        out[d] = ([rest[0]], [rest[2]])
+        out[d] = ([rest[0]], [rest[2]], [rest[0], rest[2]])
+    return out
+
+
+def runs(ranks):
+    out = []
+    for r in sorted(ranks):
+        if out and out[-1][1] == r:
+            out[-1] = (out[-1][0], r + 1)
+        else:
+            out.append((r, r + 1))
     return out
 
 
@@ -68,145 +85,168 @@ def rank_program(g, core, T, topo):
         return
     sem = T.sem
     v, s, y, t = g.vector, g.scalar, g.sync, g.tensor
-    copy = ActivationFunctionType.Copy
+    fn = ActivationFunctionType
+    copy = fn.Copy
     cores = list(T.cores)
+    near, far, peer = kinds(core, cores, topo)
     ways = plan(core, cores, topo)
     came = [plan(d, cores, topo)[core] for d in cores if d != core]
-    n_codes, n_scales = sum(len(w[0]) for w in came), sum(len(w[1]) for w in came)
+    arrivals = [sum(len(w[k]) for w in came) for k in range(3)]
 
     def wait(q, *names):
         for n in names:
             q.wait_ge(sem[n], 1)
 
+    def codes(view):
+        return view.bitcast(dt.uint32)
+
     y.dma_start(T.nwt[:, 0:4 * NW], T.nw[:]).then_inc(sem.d_nw, 16)
-    for k in range(8):
-        (y if k < 3 else s).dma_start(T.wrt[16 * k:16 * k + 16, :], T.wr[:]).then_inc(sem.d_wr, 16)
+    for k in range(2):
+        s.dma_start(T.wrt[16 * k:16 * k + 16, :], T.wr[:]).then_inc(sem.d_wr, 16)
     s.dma_start(T.plt[:], T.pl[:]).then_inc(sem.d_pl, 16)
-    for k in range(8):
+    for k in range(2):
         y.dma_start(T.wpt[16 * k:16 * k + 16, :], T.wp[:]).then_inc(sem.d_wp, 16)
-    for k in range(8):
+    for k in range(2):
         y.dma_start(T.rdt[16 * k:16 * k + 16, :], T.rd[:]).then_inc(sem.d_rd, 16)
     y.dma_start(T.pgrow[0:1, :], T.pg[:]).then_inc(sem.d_pg, 16)
     y.dma_start(T.qwt[:], T.qw[:]).then_inc(sem.d_qw, 16)
 
     fl = dict(allow_small_or_imprecise_dtypes=True)
-    g.iota(T.comp[:, 0:POOL], [[1, POOL]], 0, 0, **fl).then_inc(sem.i_comp, 1)
-    g.iota(T.cval[:], [[1, N * CW]], POOL, 0, **fl).then_inc(sem.i_val, 1)
-    g.iota(T.cdmp[:], [[16, N * CW // 16]], POOL, 1).then_inc(sem.i_dmp, 1)
-    g.iota(T.cdif[:], [[0, 16], [1, 16]], 128, -1).then_inc(sem.i_dif, 1)
     g.iota(T.crow[:], [[0, 1]], 0, 1).then_inc(sem.i_row, 1)
-
+    g.iota(T.comp[:, 0:POOL], [[1, POOL]], 0, 0, **fl).then_inc(sem.i_comp, 1)
+    g.iota(T.ccol[:], [[0, 16], [1, 16]], 0, 0, **fl).then_inc(sem.i_col, 1)
     v.memset(T.nwt[:, 4 * NW:512], 0.0).then_inc(sem.zero, 1)
-    v.wait_ge(sem.d_wr, 128)
-    v.tensor_copy(T.offw[:], T.wrt[:]).then_inc(sem.offw, 1)
+    wait(v, "i_row")
+    v.tensor_scalar(T.crow16[:], T.crow[:], 15, None, AluOpType.bitwise_and).then_inc(sem.k_row, 1)
+    v.tensor_copy(T.crowp[:], T.crow[:]).then_inc(sem.k_rowp, 1)
+    wait(v, "k_row")
+    v.tensor_copy(T.crowf[:], T.crow16[:]).then_inc(sem.k_rowf, 1)
+    wait(v, "k_rowf")
+    v.tensor_scalar(T.crown[:], T.crowf[:], -1.0, None, AluOpType.mult).then_inc(sem.k_rown, 1)
+    wait(v, "i_comp", "k_rowp")
+    odd = CW * (rank % 2)
+    pieces = [p for p in ((0, CW * rank, POOL), (CW * rank, CW * rank + CW, OWN + odd - CW * rank), (CW * rank + CW, N * CW, POOL)) if p[0] < p[1]]
+    for a, b, add in pieces:
+        v.tensor_scalar(T.cval[:, a:b], T.comp[:, a:b], float(add), None, AluOpType.add).then_inc(sem.k_val, 1)
+    v.tensor_scalar(T.cdmp[:], T.comp[:, 0:N * CW:16], T.crowp[:, 0:1], float(POOL), AluOpType.add, AluOpType.add).then_inc(sem.k_dmp, 1)
+
+    v.wait_ge(sem.d_wr, 32)
+    for k in range(4):
+        v.tensor_copy(T.offw[32 * k:32 * k + 32, :], T.wrt[:]).then_inc(sem.offw, 1)
     v.wait_ge(sem.d_nw, 16)
     wait(v, "zero")
     v.quantize_mx(T.nwq[:], T.nws[:], T.nwt[:]).then_inc(sem.q_nw, 1)
-    wait(v, "offw", "q_nw")
-    v.tensor_copy(T.slot1[:, 0:N * CW].bitcast(dt.uint32), T.nwq[:, 0:NW].bitcast(dt.uint32).indirect(T.offw[:, 0:8])).then_inc(sem.c1, 1)
-    wait(s, "offw", "q_nw")
+    v.wait_ge(sem.offw, 4)
+    wait(v, "q_nw")
+    v.tensor_copy(codes(T.slot1[:, 0:N * CW]), codes(T.nwq[:, 0:NW]).indirect(T.offw[:, 0:8])).then_inc(sem.c1, 1)
+    s.wait_ge(sem.offw, 4)
+    wait(s, "q_nw")
     s.activation(T.slot1s[:, 0:N * CW], T.nws[:, 0:NW].indirect(T.offw[:, 0:8]), copy).then_inc(sem.s1, 1)
 
-    def send(src, dst, width, base, part, arrive):
+    def send(dests, src, dst, width, base, part, bits, arrive):
         tr = []
-        for d in sorted(ways, key=lambda c: (len(ways[c][0]) == 1, c)):
+        for d in dests:
             q = T.rank_of(d)
             rid, pid = topo.addr(d, core)
             a, b = src[:, width * q:width * q + width], dst[:, base + width * rank:base + width * rank + width]
-            if part == 0:
+            if bits:
                 a, b = a.bitcast(dt.uint8), b.bitcast(dt.uint8)
             tr.append(RemoteDMATransfer(dst_ids=[DstId(rid=rid, pnc=pid)], dma_engine_mask=sum(1 << e for e in ways[d][part]),
                                         remote_sem=sem[arrive], src=a, dst=b))
         g.remote_dma_fused(tr, local_sem=sem.sent)
-        return sum(len(ways[d][part]) for d in ways)
+        return sum(len(ways[d][part]) for d in dests)
 
     sent = 0
     wait(g, "c1")
-    sent += send(T.slot1, T.win, CW, POOL, 0, "in_c1")
+    sent += send(far + near + peer, T.slot1, T.win, CW, POOL, 0, True, "in_c1")
     wait(g, "s1")
-    sent += send(T.slot1s, T.wins, CW, POOL, 1, "in_s1")
+    sent += send(far + near + peer, T.slot1s, T.wins, CW, POOL, 1, False, "in_s1")
 
-    lo = POOL + CW * rank
-    v.tensor_copy(T.offo[:, 0:1], T.wrt[:, rank:rank + 1]).then_inc(sem.offo, 1)
-    wait(v, "offo")
-    v.tensor_copy(T.win[:, lo:lo + CW].bitcast(dt.uint32), T.nwq[:, 0:NW].bitcast(dt.uint32).indirect(T.offo[:, 0:1])).then_inc(sem.own_c, 1)
-    wait(s, "offo")
-    s.activation(T.wins[:, lo:lo + CW], T.nws[:, 0:NW].indirect(T.offo[:, 0:1]), copy).then_inc(sem.own_s, 1)
+    lst = T.offw[:, rank - rank % 2:rank - rank % 2 + 2]
+    v.tensor_copy(codes(T.win[:, OWN:WIDE]), codes(T.nwq[:, 0:NW]).indirect(lst)).then_inc(sem.own_c, 1)
+    s.activation(T.wins[:, OWN:WIDE], T.nws[:, 0:NW].indirect(lst), copy).then_inc(sem.own_s, 1)
 
+    wait(s, "i_col", "k_rown")
+    s.activation(T.coff[:], T.ccol[:], fn.Square, bias=T.crown[:, 0:1]).then_inc(sem.k_coff, 1)
+    wait(s, "k_coff")
+    s.activation(T.cmask[:], T.coff[:], fn.Relu, bias=1.0, scale=-1.0).then_inc(sem.k_mask, 1)
+    s.activation(T.cnot[:], T.coff[:], fn.Sign).then_inc(sem.k_not, 1)
+    v.wait_ge(sem.d_wp, 32)
+    v.tensor_scalar(T.wpa[:], T.wpt[:], 4095, None, AluOpType.bitwise_and).then_inc(sem.k_wpa, 1)
+    wait(v, "k_wpa", "k_dmp")
+    v.tensor_tensor(T.wpb[:], T.wpa[:], T.cdmp[0:32, :], AluOpType.min).then_inc(sem.k_wpb, 1)
+    wait(v, "k_wpb")
+    for k in range(4):
+        v.tensor_copy(T.offp[32 * k:32 * k + 32, :], T.wpb[:]).then_inc(sem.k_offp, 1)
+    v.wait_ge(sem.k_val, len(pieces))
+    v.wait_ge(sem.k_offp, 4)
+    v.tensor_copy(T.comp[:, 0:512].indirect(T.offp[:, 0:8]), T.cval[:]).then_inc(sem.k_comp, 1)
+    v.wait_ge(sem.d_rd, 32)
+    for k in range(4):
+        v.tensor_scalar(T.offr[32 * k:32 * k + 32, :], T.rdt[:], 16, 15, AluOpType.mult, AluOpType.add).then_inc(sem.k_offr, 1)
+    wait(v, "k_mask", "k_comp")
+    v.tensor_tensor(T.mine[:], T.comp[:, 0:POOL], T.cmask[:], AluOpType.mult).then_inc(sem.k_mine, 1)
+    wait(v, "k_mine", "k_not")
+    v.tensor_tensor_scan(T.last[:], T.cnot[:], T.mine[:], 0.0, AluOpType.mult, AluOpType.add).then_inc(sem.k_last, 1)
+    wait(v, "k_last")
+    v.wait_ge(sem.k_offr, 4)
+    v.tensor_copy(T.list2[:], T.last[:, 0:POOL].indirect(T.offr[:, 0:2])).then_inc(sem.k_list2, 1)
     v.wait_ge(sem.d_pl, 16)
     v.quantize_mx(T.win[:, 0:POOL], T.wins[:, 0:POOL], T.plt[:]).then_inc(sem.q_pl, 1)
 
-    wait(v, "i_dmp")
-    v.wait_ge(sem.d_wp, 128)
-    v.tensor_scalar(T.wpa[:], T.wpt[:], 4095, None, AluOpType.bitwise_and).then_inc(sem.k_wpa, 1)
-    wait(v, "i_dif")
-    v.tensor_scalar(T.cmod[:], T.cdif[:], 15, None, AluOpType.bitwise_and).then_inc(sem.k_mod, 1)
-    wait(v, "k_wpa")
-    v.tensor_tensor(T.wpb[:], T.wpa[:], T.cdmp[:], AluOpType.min).then_inc(sem.k_wpb, 1)
-    wait(v, "k_mod")
-    v.tensor_scalar(T.cmask[:], T.cmod[:], 0, None, AluOpType.is_equal).then_inc(sem.k_mask, 1)
-    wait(v, "k_wpb")
-    v.tensor_copy(T.offp[:], T.wpb[:]).then_inc(sem.k_offp, 1)
-    wait(v, "i_comp", "i_val", "k_offp")
-    v.tensor_copy(T.comp[:, 0:512].indirect(T.offp[:, 0:8]), T.cval[:]).then_inc(sem.k_comp, 1)
-    wait(v, "k_mask", "k_comp")
-    v.tensor_tensor(T.fold0[:], T.comp[:, 0:POOL], T.cmask[:], AluOpType.mult).then_inc(sem.k_f0, 1)
-    wait(v, "k_f0")
-    v.tensor_tensor(T.fold1[:], T.fold0[:, 0:256:2], T.fold0[:, 1:256:2], AluOpType.add).then_inc(sem.k_f1, 1)
-    wait(v, "k_f1")
-    v.tensor_tensor(T.fold2[:], T.fold1[:, 0:128:2], T.fold1[:, 1:128:2], AluOpType.add).then_inc(sem.k_f2, 1)
-    wait(v, "k_f2")
-    v.tensor_tensor(T.fold3[:], T.fold2[:, 0:64:2], T.fold2[:, 1:64:2], AluOpType.add).then_inc(sem.k_f3, 1)
-    v.wait_ge(sem.d_rd, 128)
-    v.tensor_copy(T.offr[:], T.rdt[:]).then_inc(sem.k_offr, 1)
-    wait(v, "k_f3")
-    v.tensor_tensor(T.comp2[:], T.fold3[:, 0:32:2], T.fold3[:, 1:32:2], AluOpType.add).then_inc(sem.k_f4, 1)
-    wait(v, "k_f4", "k_offr")
-    v.tensor_copy(T.list2[:], T.comp2[:, 0:16].indirect(T.offr[:, 0:2])).then_inc(sem.k_list2, 1)
-    wait(v, "i_row")
-    v.tensor_scalar(T.crow16[:], T.crow[:], 15, None, AluOpType.bitwise_and).then_inc(sem.k_row, 1)
-    v.wait_ge(sem.d_qw, 16)
-    v.quantize_mx(T.qwq[:], T.qws[:], T.qwt[:]).then_inc(sem.q_qw, 1)
-    wait(v, "k_row")
-    v.tensor_copy(T.crowf[:], T.crow16[:]).then_inc(sem.k_rowf, 1)
-    g.wait_ge(sem.d_pg, 16)
-    g.partition_broadcast(T.pgb[:], T.pgrow[0:1, :], 128).then_inc(sem.pgb, 1)
-    wait(v, "pgb", "k_rowf")
-    v.tensor_scalar(T.off3[:], T.pgb[:], 16.0, T.crowf[:, 0:1], AluOpType.mult, AluOpType.add).then_inc(sem.k_off3, 1)
-
-    wide = POOL + N * CW
-    parts = [(a, b) for a, b in ((0, rank), (rank + 1, N)) if a < b]
+    groups = [far, near + peer]
+    picks = [runs([T.rank_of(d) for d in ds]) for ds in groups]
     wait(v, "k_list2", "q_pl", "own_c")
-    v.wait_ge(sem.in_c1, n_codes)
-    for a, b in parts:
-        v.tensor_copy(T.slot2[:, PAGE * a:PAGE * b].bitcast(dt.uint32),
-                      T.win[:, 0:wide].bitcast(dt.uint32).indirect(T.list2[:, CP * a:CP * b])).then_inc(sem.c2, 1)
+    v.wait_ge(sem.in_c1, arrivals[0])
     wait(s, "k_list2", "q_pl", "own_s")
-    s.wait_ge(sem.in_s1, n_scales)
-    for a, b in parts:
-        s.activation(T.slot2s[:, PAGE * a:PAGE * b], T.wins[:, 0:wide].indirect(T.list2[:, CP * a:CP * b]), copy).then_inc(sem.s2, 1)
-    g.wait_ge(sem.c2, len(parts))
-    sent += send(T.slot2, T.land2, PAGE, 0, 0, "in_c2")
-    g.wait_ge(sem.s2, len(parts))
-    sent += send(T.slot2s, T.land2s, PAGE, 0, 1, "in_s2")
+    s.wait_ge(sem.in_s1, arrivals[1])
+    for k in range(2):
+        for a, b in picks[k]:
+            lst = T.list2[:, CP * a:CP * b]
+            v.tensor_copy(codes(T.slot2[:, PAGE * a:PAGE * b]), codes(T.win[:, 0:WIDE]).indirect(lst)).then_inc(sem["c2_%d" % k], 1)
+            s.activation(T.slot2s[:, PAGE * a:PAGE * b], T.wins[:, 0:WIDE].indirect(lst), copy).then_inc(sem["s2_%d" % k], 1)
+    for k in range(2):
+        g.wait_ge(sem["c2_%d" % k], len(picks[k]))
+        sent += send(groups[k], T.slot2, T.land2, PAGE, 0, 2, True, "in_c2")
+    for k in range(2):
+        g.wait_ge(sem["s2_%d" % k], len(picks[k]))
+        sent += send(groups[k], T.slot2s, T.land2s, PAGE, 0, 2, False, "in_s2")
     own = (PAGE * rank, PAGE * rank + PAGE)
     lst = T.list2[:, CP * rank:CP * rank + CP]
-    v.tensor_copy(T.land2[:, own[0]:own[1]].bitcast(dt.uint32), T.win[:, 0:wide].bitcast(dt.uint32).indirect(lst)).then_inc(sem.own2_c, 1)
-    s.activation(T.land2s[:, own[0]:own[1]], T.wins[:, 0:wide].indirect(lst), copy).then_inc(sem.own2_s, 1)
+    v.tensor_copy(codes(T.land2[:, own[0]:own[1]]), codes(T.win[:, 0:WIDE]).indirect(lst)).then_inc(sem.own2_c, 1)
+    s.activation(T.land2s[:, own[0]:own[1]], T.wins[:, 0:WIDE].indirect(lst), copy).then_inc(sem.own2_s, 1)
+
+    g.wait_ge(sem.d_pg, 16)
+    g.partition_broadcast(T.pgb[:], T.pgrow[0:1, :], 128).then_inc(sem.pgb, 1)
+    v.wait_ge(sem.d_qw, 16)
+    v.quantize_mx(T.qwq[:], T.qws[:], T.qwt[:]).then_inc(sem.q_qw, 1)
+    wait(v, "pgb")
+    v.tensor_scalar(T.off3[:], T.pgb[:], 16.0, T.crowf[:, 0:1], AluOpType.mult, AluOpType.add).then_inc(sem.k_off3, 1)
+
+    def quarter(k):
+        return slice(64 * k, 64 * k + 64), T.off3[:, 4 * k:4 * k + 4]
 
     wait(v, "own2_c", "k_off3")
-    v.wait_ge(sem.in_c2, n_codes)
+    v.wait_ge(sem.in_c2, arrivals[2])
+    for k in range(4):
+        cols, lst = quarter(k)
+        v.tensor_copy(codes(T.fin[:, cols]), codes(T.land2[:, 0:N * PAGE]).indirect(lst)).then_inc(sem["fc%d" % (k // 2)], 1)
     wait(s, "own2_s", "k_off3")
-    s.wait_ge(sem.in_s2, n_scales)
+    s.wait_ge(sem.in_s2, arrivals[2])
+    wait(v, "own2_s")
+    v.wait_ge(sem.in_s2, arrivals[2])
+    for h in range(2):
+        cols, lst = quarter(2 * h)
+        s.activation(T.fins[:, cols], T.land2s[:, 0:N * PAGE].indirect(lst), copy).then_inc(sem["fs%d" % h], 1)
+        cols, lst = quarter(2 * h + 1)
+        v.tensor_copy(T.fins[:, cols], T.land2s[:, 0:N * PAGE].indirect(lst)).then_inc(sem["fs%d" % h], 1)
     wait(t, "q_qw")
     for h in range(2):
-        a, b, lst = 128 * h, 128 * h + 128, T.off3[:, 8 * h:8 * h + 8]
-        v.tensor_copy(T.fin[:, a:b].bitcast(dt.uint32), T.land2[:, 0:N * PAGE].bitcast(dt.uint32).indirect(lst)).then_inc(sem["fc%d" % h], 1)
-        s.activation(T.fins[:, a:b], T.land2s[:, 0:N * PAGE].indirect(lst), copy).then_inc(sem["fs%d" % h], 1)
-        wait(t, "fc%d" % h, "fs%d" % h)
+        t.wait_ge(sem["fc%d" % h], 2)
+        t.wait_ge(sem["fs%d" % h], 2)
         for o in range(O):
             t.matmul_mx(T.acc[:, 512 * (2 * o + h):512 * (2 * o + h) + 128], T.qwq[:, 128 * o:128 * o + 128], T.qws[:, 128 * o:128 * o + 128],
-                        T.fin[:, a:b], T.fins[:, a:b], True, True).then_inc(sem["m%d%d" % (o, h)], 1)
+                        T.fin[:, 128 * h:128 * h + 128], T.fins[:, 128 * h:128 * h + 128], True, True).then_inc(sem["m%d%d" % (o, h)], 1)
     for h in range(2):
         wait(v, "m0%d" % h)
         v.tensor_copy(T.yt[:, 128 * h:128 * h + 128], T.acc[:, 512 * h:512 * h + 128]).then_inc(sem.y0, 1)

from concourse.bass import DstId, RemoteDMATransfer
from concourse.mybir import dt, AluOpType, ActivationFunctionType

N, PG, NW, SP, CW, CP, O = 8, 16, 64, 16, 16, 4, 2
POOL = 16 * PG
PAGE = 16 * CP
OWN = POOL + N * CW
WIDE = OWN + 2 * CW
F8 = "float8_e4m3fn_x4"

SCRATCH = {
    "nwt": ("sbuf", [128, 512], "bfloat16"),
    "plt": ("sbuf", [128, 4 * POOL], "bfloat16"),
    "qwt": ("sbuf", [128, 512 * O], "bfloat16"),
    "nwq": ("sbuf", [128, 128], F8), "nws": ("sbuf", [128, 128], "uint8"),
    "qwq": ("sbuf", [128, 128 * O], F8), "qws": ("sbuf", [128, 128 * O], "uint8"),
    "slot1": ("sbuf", [128, N * CW], F8), "slot1s": ("sbuf", [128, N * CW], "uint8"),
    "win": ("sbuf", [128, WIDE], F8), "wins": ("sbuf", [128, WIDE], "uint8"),
    "slot2": ("sbuf", [128, N * PAGE], F8), "slot2s": ("sbuf", [128, N * PAGE], "uint8"),
    "land2": ("sbuf", [128, N * PAGE], F8), "land2s": ("sbuf", [128, N * PAGE], "uint8"),
    "fin": ("sbuf", [128, POOL], F8), "fins": ("sbuf", [128, POOL], "uint8"),
    "wrt": ("sbuf", [32, N * CW // 16], "int32"),
    "wpt": ("sbuf", [32, N * CW // 16], "int32"),
    "rdt": ("sbuf", [32, N * CP // 16], "int32"),
    "pgrow": ("sbuf", [1, SP], "int32"), "pgb": ("sbuf", [128, SP], "int32"),
    "cval": ("sbuf", [128, N * CW], "float32"),
    "cdmp": ("sbuf", [128, N * CW // 16], "int32"),
    "ccol": ("sbuf", [128, POOL], "float32"), "coff": ("sbuf", [128, POOL], "float32"),
    "cmask": ("sbuf", [128, POOL], "float32"), "cnot": ("sbuf", [128, POOL], "float32"),
    "crow": ("sbuf", [128, 1], "int32"), "crow16": ("sbuf", [128, 1], "int32"),
    "crowp": ("sbuf", [128, 1], "float32"), "crowf": ("sbuf", [128, 1], "float32"), "crown": ("sbuf", [128, 1], "float32"),
    "wpa": ("sbuf", [32, N * CW // 16], "int32"), "wpb": ("sbuf", [32, N * CW // 16], "int32"),
    "comp": ("sbuf", [128, 512], "float32"),
    "mine": ("sbuf", [128, POOL], "float32"), "last": ("sbuf", [128, POOL], "float32"),
    "offw": ("sbuf", [128, N * CW // 16], "uint16"),
    "offp": ("sbuf", [128, N * CW // 16], "uint16"), "offr": ("sbuf", [128, N * CP // 16], "uint16"),
    "list2": ("sbuf", [128, N * CP], "uint16"), "off3": ("sbuf", [128, SP], "uint16"),
    "acc": ("psum", [128, 512 * 4], "float32"),
    "yt": ("sbuf", [128, 256 * O], "float32"),
}
DMA_SEMS = ["d_nw", "d_wr", "d_pl", "d_wp", "d_rd", "d_pg", "d_qw", "d_y"]
EVENTS = ["zero", "offw", "q_nw", "c1", "s1", "own_c", "own_s", "q_pl", "q_qw",
          "i_comp", "i_col", "i_row", "k_val", "k_dmp", "k_coff", "k_mask", "k_not", "k_row", "k_rowp", "k_rowf", "k_rown",
          "k_wpa", "k_wpb", "k_offp", "k_comp", "k_mine", "k_last", "k_offr", "k_list2", "pgb", "k_off3",
          "c2_0", "c2_1", "s2_0", "s2_1", "own2_c", "own2_s", "fc0", "fc1", "fs0", "fs1",
          "m00", "m01", "m10", "m11", "y0", "y1"]
SEMAPHORES = DMA_SEMS + EVENTS + ["in_c1", "in_s1", "in_c2", "in_s2", "sent"]


def kinds(src, cores, topo):
    peer = [d for d in cores if d != src and d in topo.cores_of(src)]
    off = [d for d in cores if d not in topo.cores_of(src)]
    near = [d for d in off if topo.mates(src, d)] + [d for d in off if topo.same_plane(src, d)]
    return near, [d for d in off if d not in near], peer


def plan(src, cores, topo):
    near, far, peer = kinds(src, cores, topo)
    e = topo.engines(src, near[0])
    a, b = e[0::2], e[1::2]
    out = {}
    for i, d in enumerate(near):
        out[d] = ([a[i]], [b[i]], e[2 * i:2 * i + 2])
    for i, d in enumerate(far):
        out[d] = (b[2 * i:2 * i + 2], a[2 * i:2 * i + 2], e[4 * i:4 * i + 4])
    for d in peer:
        rest = [x for x in topo.engines(src, d) if x not in e]
        out[d] = ([rest[0]], [rest[2]], [rest[0], rest[2]])
    return out


def runs(ranks):
    out = []
    for r in sorted(ranks):
        if out and out[-1][1] == r:
            out[-1] = (out[-1][0], r + 1)
        else:
            out.append((r, r + 1))
    return out


def rank_program(g, core, T, topo):
    rank = T.rank_of(core)
    if rank is None:
        return
    sem = T.sem
    v, s, y, t = g.vector, g.scalar, g.sync, g.tensor
    fn = ActivationFunctionType
    copy = fn.Copy
    cores = list(T.cores)
    near, far, peer = kinds(core, cores, topo)
    ways = plan(core, cores, topo)
    came = [plan(d, cores, topo)[core] for d in cores if d != core]
    arrivals = [sum(len(w[k]) for w in came) for k in range(3)]

    def wait(q, *names):
        for n in names:
            q.wait_ge(sem[n], 1)

    def codes(view):
        return view.bitcast(dt.uint32)

    y.dma_start(T.nwt[:, 0:4 * NW], T.nw[:]).then_inc(sem.d_nw, 16)
    for k in range(2):
        s.dma_start(T.wrt[16 * k:16 * k + 16, :], T.wr[:]).then_inc(sem.d_wr, 16)
    s.dma_start(T.plt[:], T.pl[:]).then_inc(sem.d_pl, 16)
    for k in range(2):
        y.dma_start(T.wpt[16 * k:16 * k + 16, :], T.wp[:]).then_inc(sem.d_wp, 16)
    for k in range(2):
        y.dma_start(T.rdt[16 * k:16 * k + 16, :], T.rd[:]).then_inc(sem.d_rd, 16)
    y.dma_start(T.pgrow[0:1, :], T.pg[:]).then_inc(sem.d_pg, 16)
    y.dma_start(T.qwt[:], T.qw[:]).then_inc(sem.d_qw, 16)

    fl = dict(allow_small_or_imprecise_dtypes=True)
    g.iota(T.crow[:], [[0, 1]], 0, 1).then_inc(sem.i_row, 1)
    g.iota(T.comp[:, 0:POOL], [[1, POOL]], 0, 0, **fl).then_inc(sem.i_comp, 1)
    g.iota(T.ccol[:], [[0, 16], [1, 16]], 0, 0, **fl).then_inc(sem.i_col, 1)
    v.memset(T.nwt[:, 4 * NW:512], 0.0).then_inc(sem.zero, 1)
    wait(v, "i_row")
    v.tensor_scalar(T.crow16[:], T.crow[:], 15, None, AluOpType.bitwise_and).then_inc(sem.k_row, 1)
    v.tensor_copy(T.crowp[:], T.crow[:]).then_inc(sem.k_rowp, 1)
    wait(v, "k_row")
    v.tensor_copy(T.crowf[:], T.crow16[:]).then_inc(sem.k_rowf, 1)
    wait(v, "k_rowf")
    v.tensor_scalar(T.crown[:], T.crowf[:], -1.0, None, AluOpType.mult).then_inc(sem.k_rown, 1)
    wait(v, "i_comp", "k_rowp")
    odd = CW * (rank % 2)
    pieces = [p for p in ((0, CW * rank, POOL), (CW * rank, CW * rank + CW, OWN + odd - CW * rank), (CW * rank + CW, N * CW, POOL)) if p[0] < p[1]]
    for a, b, add in pieces:
        v.tensor_scalar(T.cval[:, a:b], T.comp[:, a:b], float(add), None, AluOpType.add).then_inc(sem.k_val, 1)
    v.tensor_scalar(T.cdmp[:], T.comp[:, 0:N * CW:16], T.crowp[:, 0:1], float(POOL), AluOpType.add, AluOpType.add).then_inc(sem.k_dmp, 1)

    v.wait_ge(sem.d_wr, 32)
    for k in range(4):
        v.tensor_copy(T.offw[32 * k:32 * k + 32, :], T.wrt[:]).then_inc(sem.offw, 1)
    v.wait_ge(sem.d_nw, 16)
    wait(v, "zero")
    v.quantize_mx(T.nwq[:], T.nws[:], T.nwt[:]).then_inc(sem.q_nw, 1)
    v.wait_ge(sem.offw, 4)
    wait(v, "q_nw")
    v.tensor_copy(codes(T.slot1[:, 0:N * CW]), codes(T.nwq[:, 0:NW]).indirect(T.offw[:, 0:8])).then_inc(sem.c1, 1)
    s.wait_ge(sem.offw, 4)
    wait(s, "q_nw")
    s.activation(T.slot1s[:, 0:N * CW], T.nws[:, 0:NW].indirect(T.offw[:, 0:8]), copy).then_inc(sem.s1, 1)

    def send(dests, src, dst, width, base, part, bits, arrive):
        tr = []
        for d in dests:
            q = T.rank_of(d)
            rid, pid = topo.addr(d, core)
            a, b = src[:, width * q:width * q + width], dst[:, base + width * rank:base + width * rank + width]
            if bits:
                a, b = a.bitcast(dt.uint8), b.bitcast(dt.uint8)
            tr.append(RemoteDMATransfer(dst_ids=[DstId(rid=rid, pnc=pid)], dma_engine_mask=sum(1 << e for e in ways[d][part]),
                                        remote_sem=sem[arrive], src=a, dst=b))
        g.remote_dma_fused(tr, local_sem=sem.sent)
        return sum(len(ways[d][part]) for d in dests)

    sent = 0
    wait(g, "c1")
    sent += send(far + near + peer, T.slot1, T.win, CW, POOL, 0, True, "in_c1")
    wait(g, "s1")
    sent += send(far + near + peer, T.slot1s, T.wins, CW, POOL, 1, False, "in_s1")

    lst = T.offw[:, rank - rank % 2:rank - rank % 2 + 2]
    v.tensor_copy(codes(T.win[:, OWN:WIDE]), codes(T.nwq[:, 0:NW]).indirect(lst)).then_inc(sem.own_c, 1)
    s.activation(T.wins[:, OWN:WIDE], T.nws[:, 0:NW].indirect(lst), copy).then_inc(sem.own_s, 1)

    wait(s, "i_col", "k_rown")
    s.activation(T.coff[:], T.ccol[:], fn.Square, bias=T.crown[:, 0:1]).then_inc(sem.k_coff, 1)
    wait(s, "k_coff")
    s.activation(T.cmask[:], T.coff[:], fn.Relu, bias=1.0, scale=-1.0).then_inc(sem.k_mask, 1)
    s.activation(T.cnot[:], T.coff[:], fn.Sign).then_inc(sem.k_not, 1)
    v.wait_ge(sem.d_wp, 32)
    v.tensor_scalar(T.wpa[:], T.wpt[:], 4095, None, AluOpType.bitwise_and).then_inc(sem.k_wpa, 1)
    wait(v, "k_wpa", "k_dmp")
    v.tensor_tensor(T.wpb[:], T.wpa[:], T.cdmp[0:32, :], AluOpType.min).then_inc(sem.k_wpb, 1)
    wait(v, "k_wpb")
    for k in range(4):
        v.tensor_copy(T.offp[32 * k:32 * k + 32, :], T.wpb[:]).then_inc(sem.k_offp, 1)
    v.wait_ge(sem.k_val, len(pieces))
    v.wait_ge(sem.k_offp, 4)
    v.tensor_copy(T.comp[:, 0:512].indirect(T.offp[:, 0:8]), T.cval[:]).then_inc(sem.k_comp, 1)
    v.wait_ge(sem.d_rd, 32)
    for k in range(4):
        v.tensor_scalar(T.offr[32 * k:32 * k + 32, :], T.rdt[:], 16, 15, AluOpType.mult, AluOpType.add).then_inc(sem.k_offr, 1)
    wait(v, "k_mask", "k_comp")
    v.tensor_tensor(T.mine[:], T.comp[:, 0:POOL], T.cmask[:], AluOpType.mult).then_inc(sem.k_mine, 1)
    wait(v, "k_mine", "k_not")
    v.tensor_tensor_scan(T.last[:], T.cnot[:], T.mine[:], 0.0, AluOpType.mult, AluOpType.add).then_inc(sem.k_last, 1)
    wait(v, "k_last")
    v.wait_ge(sem.k_offr, 4)
    v.tensor_copy(T.list2[:], T.last[:, 0:POOL].indirect(T.offr[:, 0:2])).then_inc(sem.k_list2, 1)
    v.wait_ge(sem.d_pl, 16)
    v.quantize_mx(T.win[:, 0:POOL], T.wins[:, 0:POOL], T.plt[:]).then_inc(sem.q_pl, 1)

    groups = [far, near + peer]
    picks = [runs([T.rank_of(d) for d in ds]) for ds in groups]
    wait(v, "k_list2", "q_pl", "own_c")
    v.wait_ge(sem.in_c1, arrivals[0])
    wait(s, "k_list2", "q_pl", "own_s")
    s.wait_ge(sem.in_s1, arrivals[1])
    for k in range(2):
        for a, b in picks[k]:
            lst = T.list2[:, CP * a:CP * b]
            v.tensor_copy(codes(T.slot2[:, PAGE * a:PAGE * b]), codes(T.win[:, 0:WIDE]).indirect(lst)).then_inc(sem["c2_%d" % k], 1)
            s.activation(T.slot2s[:, PAGE * a:PAGE * b], T.wins[:, 0:WIDE].indirect(lst), copy).then_inc(sem["s2_%d" % k], 1)
    for k in range(2):
        g.wait_ge(sem["c2_%d" % k], len(picks[k]))
        sent += send(groups[k], T.slot2, T.land2, PAGE, 0, 2, True, "in_c2")
    for k in range(2):
        g.wait_ge(sem["s2_%d" % k], len(picks[k]))
        sent += send(groups[k], T.slot2s, T.land2s, PAGE, 0, 2, False, "in_s2")
    own = (PAGE * rank, PAGE * rank + PAGE)
    lst = T.list2[:, CP * rank:CP * rank + CP]
    v.tensor_copy(codes(T.land2[:, own[0]:own[1]]), codes(T.win[:, 0:WIDE]).indirect(lst)).then_inc(sem.own2_c, 1)
    s.activation(T.land2s[:, own[0]:own[1]], T.wins[:, 0:WIDE].indirect(lst), copy).then_inc(sem.own2_s, 1)

    g.wait_ge(sem.d_pg, 16)
    g.partition_broadcast(T.pgb[:], T.pgrow[0:1, :], 128).then_inc(sem.pgb, 1)
    v.wait_ge(sem.d_qw, 16)
    v.quantize_mx(T.qwq[:], T.qws[:], T.qwt[:]).then_inc(sem.q_qw, 1)
    wait(v, "pgb")
    v.tensor_scalar(T.off3[:], T.pgb[:], 16.0, T.crowf[:, 0:1], AluOpType.mult, AluOpType.add).then_inc(sem.k_off3, 1)

    def quarter(k):
        return slice(64 * k, 64 * k + 64), T.off3[:, 4 * k:4 * k + 4]

    wait(v, "own2_c", "k_off3")
    v.wait_ge(sem.in_c2, arrivals[2])
    for k in range(4):
        cols, lst = quarter(k)
        v.tensor_copy(codes(T.fin[:, cols]), codes(T.land2[:, 0:N * PAGE]).indirect(lst)).then_inc(sem["fc%d" % (k // 2)], 1)
    wait(s, "own2_s", "k_off3")
    s.wait_ge(sem.in_s2, arrivals[2])
    wait(v, "own2_s")
    v.wait_ge(sem.in_s2, arrivals[2])
    for h in range(2):
        cols, lst = quarter(2 * h)
        s.activation(T.fins[:, cols], T.land2s[:, 0:N * PAGE].indirect(lst), copy).then_inc(sem["fs%d" % h], 1)
        cols, lst = quarter(2 * h + 1)
        v.tensor_copy(T.fins[:, cols], T.land2s[:, 0:N * PAGE].indirect(lst)).then_inc(sem["fs%d" % h], 1)
    wait(t, "q_qw")
    for h in range(2):
        t.wait_ge(sem["fc%d" % h], 2)
        t.wait_ge(sem["fs%d" % h], 2)
        for o in range(O):
            t.matmul_mx(T.acc[:, 512 * (2 * o + h):512 * (2 * o + h) + 128], T.qwq[:, 128 * o:128 * o + 128], T.qws[:, 128 * o:128 * o + 128],
                        T.fin[:, 128 * h:128 * h + 128], T.fins[:, 128 * h:128 * h + 128], True, True).then_inc(sem["m%d%d" % (o, h)], 1)
    for h in range(2):
        wait(v, "m0%d" % h)
        v.tensor_copy(T.yt[:, 128 * h:128 * h + 128], T.acc[:, 512 * h:512 * h + 128]).then_inc(sem.y0, 1)
        wait(s, "m1%d" % h)
        s.activation(T.yt[:, 256 + 128 * h:256 + 128 * h + 128], T.acc[:, 1024 + 512 * h:1024 + 512 * h + 128], copy).then_inc(sem.y1, 1)
    y.wait_ge(sem.y0, 2)
    y.dma_start(T.y[:, 0:256], T.yt[:, 0:256]).then_inc(sem.d_y, 16)
    s.wait_ge(sem.y1, 2)
    s.dma_start(T.y[:, 256:512], T.yt[:, 256:512]).then_inc(sem.d_y, 16)
    y.wait_ge(sem.d_y, 32)
    g.wait_ge(sem.sent, sent)
